import numpy as np
import ml_dtypes


def mxq(x, axis, fmt="e4m3"):
    dtype, down = {"e4m3": (ml_dtypes.float8_e4m3fn, 7), "e5m2": (ml_dtypes.float8_e5m2, 14)}[fmt]
    v = np.moveaxis(np.asarray(x, np.float32).astype(ml_dtypes.bfloat16).astype(np.float64), axis, -1)
    blocks = v.reshape(v.shape[:-1] + (-1, 32))
    amax = np.abs(blocks).max(-1, keepdims=True)
    byte = np.maximum(np.where(amax > 0, np.frexp(amax)[1] - 1 + 127, 0) - down, 1)
    scale = np.exp2(byte - 127.0)
    codes = (blocks / scale).astype(np.float32).astype(dtype).astype(np.float64)
    return np.moveaxis((codes * scale).reshape(v.shape), -1, axis)


WIDE = False


def mx_kscale(k):
    if not WIDE:
        return np.ones(k)
    levels = np.array([10, -10, 5, -5, 0])
    if k % 512:
        return np.exp2(np.random.permutation(np.resize(levels, k // 32))).repeat(32)
    a = np.empty((k // 512, 16))
    for p in range(k // 512):
        a[p, :8] = np.random.permutation(np.resize(levels, 8))
        for g in range(8):
            far = levels[np.abs(levels - a[p, g]) >= 10]
            a[p, g + 8] = far[np.random.randint(len(far))]
    return np.exp2(a.ravel()).repeat(32)


def f64(x):
    return np.asarray(x).astype(np.float64)


def striped(idx):
    return np.tile(idx.reshape(-1, 16).T, (8, 1)).astype(np.uint16)


def unstriped(offs):
    return offs[:16].T.reshape(-1).astype(np.int64)


def pack_weight(w):
    k, n = w.shape
    w = f64(np.asarray(w, np.float32).astype(ml_dtypes.bfloat16)).reshape(k // 32, 32, n)
    amax = np.abs(w).max(1)
    byte = np.clip(np.where(amax > 0, np.frexp(amax)[1] - 1 + 127 - 7, 1), 1, 254)
    scaled = (w * np.exp2(127.0 - byte)[:, None, :]).reshape(k, n).astype(np.float32)
    words = np.ascontiguousarray(scaled.reshape(k // 512, 128, 4, n).transpose(0, 1, 3, 2)).astype(ml_dtypes.float8_e4m3fn).view(np.uint8)
    return words, np.ascontiguousarray(byte.astype(np.uint8).reshape(k // 512, 16, n))


def unpack_weight(words, scales):
    g, p, n, _ = words.shape
    vals = np.ascontiguousarray(words).view(ml_dtypes.float8_e4m3fn).astype(np.float64) * np.repeat(np.exp2(scales.astype(np.float64) - 127.0), 8, axis=1)[..., None]
    return vals.transpose(0, 1, 3, 2).reshape(g * 512, n)


def silu(v):
    return v / (1.0 + np.exp(-np.maximum(v, -700.0)))


K, T, D, S, V, N = 1024, 2048, 3, 512, 256, 512


def setup_inputs():
    n = np.random.standard_normal
    s = mx_kscale(K)[:, None]
    packed = pack_weight(n((K, T)) * s)
    return {
        "x_words": packed[0],
        "x_scales": packed[1],
        "w": (n((K, N)) / np.sqrt(K) / s).astype(np.float32),
        "b": (0.3 * n((N, 1))).astype(np.float32),
        "gate": np.tile(np.random.uniform(0.2, 1.0, (D, 1, V)) / np.sqrt(D), (1, N, 1)).astype(np.float32),
        "offs": striped(np.random.permutation(T)[:S]),
        "pos1": striped(np.random.permutation(S)[:V]),
        "pos2": striped(np.random.permutation(S)[:V]),
        "pos3": striped(np.random.permutation(S)[:V]),
    }


def reference(x_words, x_scales, w, b, gate, offs, pos1, pos2, pos3):
    idx = unstriped(offs)
    xq = unpack_weight(x_words, x_scales)[:, idx]
    y = mxq(f64(w), 0, "e4m3").T @ xq
    y = silu(y + f64(b))
    return sum(f64(gate[d]) * y[:, unstriped(p)] for d, p in enumerate((pos1, pos2, pos3)))

@@ -1,0 +1,136 @@
+from contextlib import ExitStack
+
+import concourse.mybir as mybir
+from concourse.masks import make_identity
+
+K, T, D, S, V, N = 1024, 2048, 3, 512, 256, 512
+FLOPS = 2 * K * N * S
+P = 128
+PACK = 4
+PASSES = K // (P * PACK)
+BLOCKS = N // P
+
+F32 = mybir.dt.float32
+BF16 = mybir.dt.bfloat16
+I32 = mybir.dt.int32
+U32 = mybir.dt.uint32
+U16 = mybir.dt.uint16
+U8 = mybir.dt.uint8
+FP8X4 = mybir.dt.float8_e4m3fn_x4
+ACT = mybir.ActivationFunctionType
+ALU = mybir.AluOpType
+
+
+def tile_picked_sub_lin_silu_sub_p_kernel(tc, x_words, x_scales, w, b, gate, offs, pos1, pos2, pos3, out):
+    nc = tc.nc
+    with ExitStack() as ctx:
+        lists = ctx.enter_context(tc.tile_pool(name="lists", bufs=1))
+        keep = ctx.enter_context(tc.tile_pool(name="keep", bufs=1))
+        psum = ctx.enter_context(tc.psum_pool(name="psum", bufs=1))
+
+        node_list = lists.tile([P, S // 16], U16, name="node_list")
+        nbr_lists = [lists.tile([P, V // 16], U16, name=f"nbr_list{d}") for d in range(D)]
+
+        x_tab = [keep.tile([P, T], I32, name=f"x_tab{o}", align_bytes=64) for o in range(PASSES)]
+        s_tab = keep.tile([P, T], U8, name="s_tab", align_bytes=64)
+        w_raw = [[keep.tile([P, PACK, P], F32, name=f"w_raw{i}_{o}", align_bytes=64) for o in range(PASSES)] for i in range(BLOCKS)]
+        gates = keep.tile([P, D, V], F32, name="gates", align_bytes=64)
+        bias_rows = keep.tile([P, P], F32, name="bias_rows", align_bytes=64)
+        ident = keep.tile([P, P], F32, name="ident", align_bytes=64)
+        warm_in = keep.tile([P, 8], F32, name="warm_in")
+        warm_out = keep.tile([P, 8], F32, name="warm_out")
+
+        def load_x(o):
+            nc.sync.dma_start(x_tab[o][:], x_words[o].rearrange("p n t -> p (n t)").bitcast(I32))
+
+        def load_w(i):
+            for o in range(PASSES):
+                rows = w[o * P * PACK : (o + 1) * P * PACK, i * P : (i + 1) * P]
+                nc.sync.dma_start(w_raw[i][o][:], rows.rearrange("(p j) c -> p j c", j=PACK))
+
+        nc.vector.memset(warm_in[:], 0.0)
+        nc.scalar.activation(warm_out[:], warm_in[:], ACT.Silu)
+
+        nc.gpsimd.memset(s_tab[:].bitcast(I32), 0)
+        for q in range(4):
+            nc.gpsimd.dma_start(
+                s_tab[32 * q : 32 * q + 4 * PASSES, :].bitcast(I32),
+                x_scales[:, 4 * q : 4 * q + 4, :].bitcast(I32),
+            )
+        nc.vector.memset(bias_rows[:], 0.0)
+        nc.scalar.dma_start(bias_rows[0:BLOCKS, :], b.rearrange("(i p) one -> i (p one)", p=P))
+        make_identity(nc, ident[:])
+
+        load_x(0)
+        nc.sync.dma_start(node_list[:], offs)
+        load_w(0)
+        load_x(1)
+        load_w(1)
+        nc.sync.dma_start(gates[:], gate[:, 0:P, :].rearrange("d p v -> p d v"))
+        for d, pos in enumerate((pos1, pos2, pos3)):
+            nc.sync.dma_start(nbr_lists[d][:], pos)
+        load_w(2)
+        load_w(3)
+
+        bias_ps = psum.tile([P, P], F32, name="bias_ps")
+        nc.tensor.transpose(bias_ps[:], bias_rows[:], ident[:])
+        bias = keep.tile([P, BLOCKS], F32, name="bias")
+        nc.scalar.copy(bias[:], bias_ps[:, 0:BLOCKS])
+
+        x_codes = [keep.tile([P, S], U32, name=f"x_codes{o}", align_bytes=64) for o in range(PASSES)]
+        x_bytes = keep.tile([P, S], U8, name="x_bytes", align_bytes=64)
+        nc.vector.tensor_copy(x_codes[0][:], x_tab[0][:].bitcast(U32).indirect(node_list[:]))
+        nc.vector.tensor_copy(x_bytes[:], s_tab[:].indirect(node_list[:]))
+
+        def cast_w(i):
+            grouped = keep.tile([P, PASSES, P, PACK], BF16, name=f"grouped{i}", align_bytes=64)
+            for o in range(PASSES):
+                nc.scalar.copy(
+                    grouped[:, o, :, :].rearrange("p (c e) j -> p c j e", e=4),
+                    w_raw[i][o][:].rearrange("p j (c e) -> p c j e", e=4),
+                )
+            return grouped
+
+        def quantize_w(i, grouped):
+            codes = keep.tile([P, PASSES * P], U32, name=f"w_codes{i}", align_bytes=64)
+            scales = keep.tile([P, PASSES * P], U8, name=f"w_scales{i}", align_bytes=64)
+            nc.vector.quantize_mx(
+                out=codes[:].bitcast(FP8X4), scales=scales[:], in_=grouped[:].rearrange("p o c j -> p (o c j)")
+            )
+            return codes, scales
+
+        def product(i, codes, scales):
+            acc = psum.tile([P, S], F32, name=f"acc{i}")
+            for o in range(PASSES):
+                cols = slice(o * P, (o + 1) * P)
+                nc.tensor.matmul_mx(
+                    out=acc[:],
+                    lhsT=codes[:, cols].bitcast(FP8X4),
+                    lhsT_scale=scales[:, cols],
+                    rhs=x_codes[o][:].bitcast(FP8X4),
+                    rhs_scale=x_bytes[4 * o :, :],
+                    start=(o == 0),
+                    stop=(o == PASSES - 1),
+                )
+            y = keep.tile([P, S], F32, name=f"y{i}", align_bytes=64)
+            nc.scalar.activation(y[:], acc[:], ACT.Silu, bias=bias[:, i : i + 1])
+            return y
+
+        def neighbours(i, y):
+            terms = [keep.tile([P, V], F32, name=f"term{i}_{d}") for d in range(D)]
+            for d in range(D):
+                nc.vector.tensor_tensor(terms[d][:], y[:].indirect(nbr_lists[d][:]), gates[:, d, :], ALU.mult)
+            part = keep.tile([P, V], F32, name=f"part{i}")
+            nc.vector.tensor_tensor(part[:], terms[0][:], terms[1][:], ALU.add)
+            res = keep.tile([P, V], F32, name=f"res{i}")
+            nc.vector.tensor_tensor(res[:], part[:], terms[2][:], ALU.add)
+            nc.sync.dma_start(out[i * P : (i + 1) * P, :], res[:])
+
+        quantized = quantize_w(0, cast_w(0))
+        nc.vector.tensor_copy(x_codes[1][:], x_tab[1][:].bitcast(U32).indirect(node_list[:]))
+        y = product(0, *quantized)
+        for i in range(BLOCKS):
+            y_now = y
+            if i + 1 < BLOCKS:
+                y = product(i + 1, *quantize_w(i + 1, cast_w(i + 1)))
+            neighbours(i, y_now)

@@ -1,7 +1,6 @@
 from contextlib import ExitStack
 
 import concourse.mybir as mybir
-from concourse.masks import make_identity
 
 K, T, D, S, V, N = 1024, 2048, 3, 512, 256, 512
 FLOPS = 2 * K * N * S
@@ -9,6 +8,7 @@ P = 128
 PACK = 4
 PASSES = K // (P * PACK)
 BLOCKS = N // P
+HALVES = V // P
 
 F32 = mybir.dt.float32
 BF16 = mybir.dt.bfloat16
@@ -26,111 +26,198 @@ def tile_picked_sub_lin_silu_sub_p_kernel(tc, x_words, x_scales, w, b, gate, off
     with ExitStack() as ctx:
         lists = ctx.enter_context(tc.tile_pool(name="lists", bufs=1))
         keep = ctx.enter_context(tc.tile_pool(name="keep", bufs=1))
-        psum = ctx.enter_context(tc.psum_pool(name="psum", bufs=1))
+        sums = ctx.enter_context(tc.psum_pool(name="sums", bufs=1))
+        turns = ctx.enter_context(tc.psum_pool(name="turns", bufs=5))
+
+        def sbuf(shape, dtype, name, tag=None):
+            return keep.tile(shape, dtype, name=name, tag=tag or name, align_bytes=64)
 
         node_list = lists.tile([P, S // 16], U16, name="node_list")
         nbr_lists = [lists.tile([P, V // 16], U16, name=f"nbr_list{d}") for d in range(D)]
 
-        x_tab = [keep.tile([P, T], I32, name=f"x_tab{o}", align_bytes=64) for o in range(PASSES)]
-        s_tab = keep.tile([P, T], U8, name="s_tab", align_bytes=64)
-        w_raw = [[keep.tile([P, PACK, P], F32, name=f"w_raw{i}_{o}", align_bytes=64) for o in range(PASSES)] for i in range(BLOCKS)]
-        gates = keep.tile([P, D, V], F32, name="gates", align_bytes=64)
-        bias_rows = keep.tile([P, P], F32, name="bias_rows", align_bytes=64)
-        ident = keep.tile([P, P], F32, name="ident", align_bytes=64)
-        warm_in = keep.tile([P, 8], F32, name="warm_in")
-        warm_out = keep.tile([P, 8], F32, name="warm_out")
+        x_tab = [sbuf([P, T], I32, f"x_tab{o}") for o in range(PASSES)]
+        s_tab = sbuf([P, T], U8, "s_tab")
+        w_raw = [[sbuf([P, PACK, P], F32, f"w_raw{i}_{o}") for o in range(PASSES)] for i in range(BLOCKS)]
+        gates = sbuf([P, D, V], F32, "gates")
+        bias_rows = sbuf([P, P], F32, "bias_rows")
+        ident = sbuf([P, P], F32, "ident")
+        warm_in = sbuf([P, 8], F32, "warm_in")
+        warm_out = sbuf([P, 8], F32, "warm_out")
 
         def load_x(o):
             nc.sync.dma_start(x_tab[o][:], x_words[o].rearrange("p n t -> p (n t)").bitcast(I32))
 
-        def load_w(i):
-            for o in range(PASSES):
-                rows = w[o * P * PACK : (o + 1) * P * PACK, i * P : (i + 1) * P]
-                nc.sync.dma_start(w_raw[i][o][:], rows.rearrange("(p j) c -> p j c", j=PACK))
+        def load_w(i, o):
+            src = w[o * P * PACK : (o + 1) * P * PACK, i * P : (i + 1) * P]
+            nc.sync.dma_start(w_raw[i][o][:], src.rearrange("(p j) c -> p j c", j=PACK))
 
-        nc.vector.memset(warm_in[:], 0.0)
-        nc.scalar.activation(warm_out[:], warm_in[:], ACT.Silu)
+        def load_list(d):
+            nc.sync.dma_start(nbr_lists[d][:], (pos1, pos2, pos3)[d])
 
         nc.gpsimd.memset(s_tab[:].bitcast(I32), 0)
         for q in range(4):
-            nc.gpsimd.dma_start(
+            nc.scalar.dma_start(
                 s_tab[32 * q : 32 * q + 4 * PASSES, :].bitcast(I32),
                 x_scales[:, 4 * q : 4 * q + 4, :].bitcast(I32),
             )
+        nc.vector.memset(warm_in[:], 0.0)
+        nc.scalar.activation(warm_out[:], warm_in[:], ACT.Silu)
         nc.vector.memset(bias_rows[:], 0.0)
-        nc.scalar.dma_start(bias_rows[0:BLOCKS, :], b.rearrange("(i p) one -> i (p one)", p=P))
-        make_identity(nc, ident[:])
+        nc.gpsimd.dma_start(bias_rows[0:BLOCKS, :], b.rearrange("(i p) one -> i (p one)", p=P))
 
-        load_x(0)
+        ones = sbuf([P, P], F32, "ones")
+        base = sbuf([P, 1], F32, "base")
+        ramp = sbuf([P, P], F32, "ramp")
+        lane = sbuf([P, 32], F32, "lane")
+        nc.vector.memset(ones[:], 1.0)
+        for q in range(4):
+            nc.vector.memset(base[32 * q : 32 * (q + 1), :], 32.0 * q)
+        nc.vector.tensor_tensor_scan(ramp[:], ones[:], ones[:], 0.0, ALU.mult, ALU.add)
+        nc.vector.transpose(lane[:], ramp[:, 0:32])
+        nc.vector.tensor_scalar(ident[:], ramp[:], base[:], lane[:, 0:1], ALU.subtract, ALU.is_equal)
+
+        load_w(0, 0)
         nc.sync.dma_start(node_list[:], offs)
-        load_w(0)
+        load_w(0, 1)
+        load_list(0)
+        load_list(1)
+        load_x(0)
+        load_list(2)
         load_x(1)
-        load_w(1)
+        load_w(1, 0)
+        load_w(1, 1)
         nc.sync.dma_start(gates[:], gate[:, 0:P, :].rearrange("d p v -> p d v"))
-        for d, pos in enumerate((pos1, pos2, pos3)):
-            nc.sync.dma_start(nbr_lists[d][:], pos)
-        load_w(2)
-        load_w(3)
-
-        bias_ps = psum.tile([P, P], F32, name="bias_ps")
-        nc.tensor.transpose(bias_ps[:], bias_rows[:], ident[:])
-        bias = keep.tile([P, BLOCKS], F32, name="bias")
-        nc.scalar.copy(bias[:], bias_ps[:, 0:BLOCKS])
-
-        x_codes = [keep.tile([P, S], U32, name=f"x_codes{o}", align_bytes=64) for o in range(PASSES)]
-        x_bytes = keep.tile([P, S], U8, name="x_bytes", align_bytes=64)
-        nc.vector.tensor_copy(x_codes[0][:], x_tab[0][:].bitcast(U32).indirect(node_list[:]))
-        nc.vector.tensor_copy(x_bytes[:], s_tab[:].indirect(node_list[:]))
-
-        def cast_w(i):
-            grouped = keep.tile([P, PASSES, P, PACK], BF16, name=f"grouped{i}", align_bytes=64)
+        for i in range(2, BLOCKS):
             for o in range(PASSES):
-                nc.scalar.copy(
-                    grouped[:, o, :, :].rearrange("p (c e) j -> p c j e", e=4),
-                    w_raw[i][o][:].rearrange("p j (c e) -> p c j e", e=4),
-                )
-            return grouped
+                load_w(i, o)
 
-        def quantize_w(i, grouped):
-            codes = keep.tile([P, PASSES * P], U32, name=f"w_codes{i}", align_bytes=64)
-            scales = keep.tile([P, PASSES * P], U8, name=f"w_scales{i}", align_bytes=64)
-            nc.vector.quantize_mx(
-                out=codes[:].bitcast(FP8X4), scales=scales[:], in_=grouped[:].rearrange("p o c j -> p (o c j)")
+        x_codes = [sbuf([P, S], U32, "x_codes0"), sbuf([P, S], U32, "x_codes1", "s_tab")]
+        x_bytes = sbuf([P, S], U8, "x_bytes")
+        w_codes = [sbuf([P, PASSES * P], U32, f"w_codes{i}") for i in range(BLOCKS)]
+        w_bytes = [sbuf([P, PASSES * P], U8, f"w_bytes{i}") for i in range(BLOCKS)]
+        homes = ["grouped0", "x_tab1", "w_codes0", "w_codes1"]
+        grouped = [sbuf([P, PASSES, P, PACK], BF16, f"grouped{i}", homes[i]) for i in range(BLOCKS)]
+
+        def cast_w(i, o, copy):
+            copy(
+                grouped[i][:, o, :, :].rearrange("p (c e) j -> p c j e", e=4),
+                w_raw[i][o][:].rearrange("p j (c e) -> p c j e", e=4),
             )
-            return codes, scales
 
-        def product(i, codes, scales):
-            acc = psum.tile([P, S], F32, name=f"acc{i}")
+        def quantize_w(i):
+            nc.vector.quantize_mx(
+                out=w_codes[i][:].bitcast(FP8X4),
+                scales=w_bytes[i][:],
+                in_=grouped[i][:].rearrange("p o c j -> p (o c j)"),
+            )
+
+        def mx_pass(acc, i, o, entries):
+            cols = slice(o * P, (o + 1) * P)
+            nc.tensor.matmul_mx(
+                out=acc,
+                lhsT=w_codes[i][:, cols].bitcast(FP8X4),
+                lhsT_scale=w_bytes[i][:, cols],
+                rhs=x_codes[o][:, entries].bitcast(FP8X4),
+                rhs_scale=x_bytes[4 * o :, entries],
+                start=(o == 0),
+                stop=(o == PASSES - 1),
+            )
+
+        def product(i):
+            acc = sums.tile([P, S], F32, name=f"acc{i}", tag=f"bank{(i + 1) % 3}")
             for o in range(PASSES):
-                cols = slice(o * P, (o + 1) * P)
-                nc.tensor.matmul_mx(
-                    out=acc[:],
-                    lhsT=codes[:, cols].bitcast(FP8X4),
-                    lhsT_scale=scales[:, cols],
-                    rhs=x_codes[o][:].bitcast(FP8X4),
-                    rhs_scale=x_bytes[4 * o :, :],
-                    start=(o == 0),
-                    stop=(o == PASSES - 1),
-                )
-            y = keep.tile([P, S], F32, name=f"y{i}", align_bytes=64)
+                mx_pass(acc[:], i, o, slice(0, S))
+            return acc
+
+        def silu(i, acc, home=None):
+            y = sbuf([P, S], F32, f"y{i}", home)
             nc.scalar.activation(y[:], acc[:], ACT.Silu, bias=bias[:, i : i + 1])
             return y
 
-        def neighbours(i, y):
-            terms = [keep.tile([P, V], F32, name=f"term{i}_{d}") for d in range(D)]
+        def fetch(i, y, home):
+            terms = []
             for d in range(D):
-                nc.vector.tensor_tensor(terms[d][:], y[:].indirect(nbr_lists[d][:]), gates[:, d, :], ALU.mult)
-            part = keep.tile([P, V], F32, name=f"part{i}")
-            nc.vector.tensor_tensor(part[:], terms[0][:], terms[1][:], ALU.add)
-            res = keep.tile([P, V], F32, name=f"res{i}")
-            nc.vector.tensor_tensor(res[:], part[:], terms[2][:], ALU.add)
+                term = sbuf([P, V], F32, f"term{i}_{d}", home.get(d))
+                nc.vector.tensor_tensor(term[:], y[:].indirect(nbr_lists[d][:]), gates[:, d, :], ALU.mult)
+                terms.append(term)
+            return terms
+
+        def add_on_vector(i, terms):
+            cols = [slice(h * P, (h + 1) * P) for h in range(HALVES)]
+            part = sbuf([P, V], F32, f"part{i}")
+            for c in cols:
+                nc.vector.tensor_tensor(part[:, c], terms[0][:, c], terms[1][:, c], ALU.add)
+            res = sbuf([P, V], F32, f"res{i}")
+            for c in cols:
+                nc.vector.tensor_tensor(res[:, c], part[:, c], terms[2][:, c], ALU.add)
+                nc.sync.dma_start(out[i * P : (i + 1) * P, c], res[:, c])
+
+        def add_on_tensor(i, terms):
+            turned = (sums.tile([P, HALVES, P], F32, name=f"turned{i}", tag="bank2") if i == 0 else turns.tile([P, HALVES, P], F32, name=f"turned{i}", tag="turns"))
+            for h in range(HALVES):
+                for d in range(D):
+                    nc.tensor.matmul(
+                        turned[:, h, :],
+                        terms[d][:, h * P : (h + 1) * P],
+                        ident[:],
+                        is_transpose=True,
+                        start=(d == 0),
+                        stop=(d == D - 1),
+                    )
+            staged = sbuf([P, HALVES, P], F32, f"staged{i}")
+            nc.scalar.copy(staged[:], turned[:])
+            back = turns.tile([P, V], F32, name=f"back{i}", tag="turns")
+            for h in range(HALVES):
+                nc.tensor.transpose(back[:, h * P : (h + 1) * P], staged[:, h, :], ident[:])
+            res = sbuf([P, V], F32, f"res{i}")
+            nc.scalar.copy(res[:], back[:])
             nc.sync.dma_start(out[i * P : (i + 1) * P, :], res[:])
 
-        quantized = quantize_w(0, cast_w(0))
-        nc.vector.tensor_copy(x_codes[1][:], x_tab[1][:].bitcast(U32).indirect(node_list[:]))
-        y = product(0, *quantized)
-        for i in range(BLOCKS):
-            y_now = y
-            if i + 1 < BLOCKS:
-                y = product(i + 1, *quantize_w(i + 1, cast_w(i + 1)))
-            neighbours(i, y_now)
+        for o in range(PASSES):
+            cast_w(0, o, nc.scalar.copy)
+        quantize_w(0)
+        nc.vector.tensor_copy(x_codes[0][:], x_tab[0][:].bitcast(U32).indirect(node_list[:]))
+        nc.vector.tensor_copy(x_bytes[:], s_tab[:].indirect(node_list[:]))
+
+        bias_t = turns.tile([P, P], F32, name="bias_t", tag="turns")
+        nc.tensor.transpose(bias_t[:], bias_rows[:], ident[:])
+        bias = sbuf([P, BLOCKS], F32, "bias")
+        nc.scalar.copy(bias[:], bias_t[:, 0:BLOCKS])
+
+        half = S // 2
+        first = [sums.tile([P, half], F32, name=f"first{u}", tag=f"bank{u}") for u in range(2)]
+        for u in range(2):
+            mx_pass(first[u][:], 0, 0, slice(u * half, (u + 1) * half))
+        y0 = sbuf([P, S], F32, "y0")
+        for u in range(2):
+            entries = slice(u * half, (u + 1) * half)
+            nc.vector.tensor_copy(
+                x_codes[1][:, entries],
+                x_tab[1][:].bitcast(U32).indirect(node_list[:, u * half // 16 : (u + 1) * half // 16]),
+            )
+            mx_pass(first[u][:], 0, 1, entries)
+            nc.scalar.activation(y0[:, entries], first[u][:], ACT.Silu, bias=bias[:, 0:1])
+        cast_w(1, 0, nc.scalar.copy)
+        cast_w(1, 1, nc.vector.tensor_copy)
+        quantize_w(1)
+        acc1 = product(1)
+
+        for o in range(PASSES):
+            cast_w(2, o, nc.scalar.copy)
+        y1 = silu(1, acc1, "w_raw2_1")
+        terms0 = fetch(0, y0, {0: homes[1]})
+        quantize_w(2)
+        acc2 = product(2)
+        for o in range(PASSES):
+            cast_w(3, o, nc.scalar.copy)
+        quantize_w(3)
+        y2 = silu(2, acc2)
+        acc3 = product(3)
+        terms1 = fetch(1, y1, {0: homes[2], 2: homes[3]})
+        y3 = silu(3, acc3)
+        add_on_tensor(0, terms0)
+        terms2 = fetch(2, y2, {})
+        add_on_tensor(1, terms1)
+        terms3 = fetch(3, y3, {})
+        add_on_tensor(2, terms2)
+        add_on_vector(3, terms3)

from contextlib import ExitStack

import concourse.mybir as mybir

K, T, D, S, V, N = 1024, 2048, 3, 512, 256, 512
FLOPS = 2 * K * N * S
P = 128
PACK = 4
PASSES = K // (P * PACK)
BLOCKS = N // P
HALVES = V // P

F32 = mybir.dt.float32
BF16 = mybir.dt.bfloat16
I32 = mybir.dt.int32
U32 = mybir.dt.uint32
U16 = mybir.dt.uint16
U8 = mybir.dt.uint8
FP8X4 = mybir.dt.float8_e4m3fn_x4
ACT = mybir.ActivationFunctionType
ALU = mybir.AluOpType


def tile_picked_sub_lin_silu_sub_p_kernel(tc, x_words, x_scales, w, b, gate, offs, pos1, pos2, pos3, out):
    nc = tc.nc
    with ExitStack() as ctx:
        lists = ctx.enter_context(tc.tile_pool(name="lists", bufs=1))
        keep = ctx.enter_context(tc.tile_pool(name="keep", bufs=1))
        sums = ctx.enter_context(tc.psum_pool(name="sums", bufs=1))
        turns = ctx.enter_context(tc.psum_pool(name="turns", bufs=5))

        def sbuf(shape, dtype, name, tag=None):
            return keep.tile(shape, dtype, name=name, tag=tag or name, align_bytes=64)

        node_list = lists.tile([P, S // 16], U16, name="node_list")
        nbr_lists = [lists.tile([P, V // 16], U16, name=f"nbr_list{d}") for d in range(D)]

        x_tab = [sbuf([P, T], I32, f"x_tab{o}") for o in range(PASSES)]
        s_tab = sbuf([P, T], U8, "s_tab")
        w_raw = [[sbuf([P, PACK, P], F32, f"w_raw{i}_{o}") for o in range(PASSES)] for i in range(BLOCKS)]
        gates = sbuf([P, D, V], F32, "gates")
        bias_rows = sbuf([P, P], F32, "bias_rows")
        ident = sbuf([P, P], F32, "ident")
        warm_in = sbuf([P, 8], F32, "warm_in")
        warm_out = sbuf([P, 8], F32, "warm_out")

        def load_x(o):
            nc.sync.dma_start(x_tab[o][:], x_words[o].rearrange("p n t -> p (n t)").bitcast(I32))

        def load_w(i, o):
            src = w[o * P * PACK : (o + 1) * P * PACK, i * P : (i + 1) * P]
            nc.sync.dma_start(w_raw[i][o][:], src.rearrange("(p j) c -> p j c", j=PACK))

        def load_list(d):
            nc.sync.dma_start(nbr_lists[d][:], (pos1, pos2, pos3)[d])

        nc.gpsimd.memset(s_tab[:].bitcast(I32), 0)
        for q in range(4):
            nc.scalar.dma_start(
                s_tab[32 * q : 32 * q + 4 * PASSES, :].bitcast(I32),
                x_scales[:, 4 * q : 4 * q + 4, :].bitcast(I32),
            )
        nc.vector.memset(warm_in[:], 0.0)
        nc.scalar.activation(warm_out[:], warm_in[:], ACT.Silu)
        nc.vector.memset(bias_rows[:], 0.0)
        nc.gpsimd.dma_start(bias_rows[0:BLOCKS, :], b.rearrange("(i p) one -> i (p one)", p=P))

        ones = sbuf([P, P], F32, "ones")
        base = sbuf([P, 1], F32, "base")
        ramp = sbuf([P, P], F32, "ramp")
        lane = sbuf([P, 32], F32, "lane")
        nc.vector.memset(ones[:], 1.0)
        for q in range(4):
            nc.vector.memset(base[32 * q : 32 * (q + 1), :], 32.0 * q)
        nc.vector.tensor_tensor_scan(ramp[:], ones[:], ones[:], 0.0, ALU.mult, ALU.add)
        nc.vector.transpose(lane[:], ramp[:, 0:32])
        nc.vector.tensor_scalar(ident[:], ramp[:], base[:], lane[:, 0:1], ALU.subtract, ALU.is_equal)

        load_w(0, 0)
        nc.sync.dma_start(node_list[:], offs)
        load_w(0, 1)
        load_list(0)
        load_list(1)
        load_x(0)
        load_list(2)
        load_x(1)
        load_w(1, 0)
        load_w(1, 1)
        nc.sync.dma_start(gates[:], gate[:, 0:P, :].rearrange("d p v -> p d v"))
        for i in range(2, BLOCKS):
            for o in range(PASSES):
                load_w(i, o)

        x_codes = [sbuf([P, S], U32, "x_codes0"), sbuf([P, S], U32, "x_codes1", "s_tab")]
        x_bytes = sbuf([P, S], U8, "x_bytes")
        w_codes = [sbuf([P, PASSES * P], U32, f"w_codes{i}") for i in range(BLOCKS)]
        w_bytes = [sbuf([P, PASSES * P], U8, f"w_bytes{i}") for i in range(BLOCKS)]
        homes = ["grouped0", "x_tab1", "w_codes0", "w_codes1"]
        grouped = [sbuf([P, PASSES, P, PACK], BF16, f"grouped{i}", homes[i]) for i in range(BLOCKS)]

        def cast_w(i, o, copy):
            copy(
                grouped[i][:, o, :, :].rearrange("p (c e) j -> p c j e", e=4),
                w_raw[i][o][:].rearrange("p j (c e) -> p c j e", e=4),
            )

        def quantize_w(i):
            nc.vector.quantize_mx(
                out=w_codes[i][:].bitcast(FP8X4),
                scales=w_bytes[i][:],
                in_=grouped[i][:].rearrange("p o c j -> p (o c j)"),
            )

        def mx_pass(acc, i, o, entries):
            cols = slice(o * P, (o + 1) * P)
            nc.tensor.matmul_mx(
                out=acc,
                lhsT=w_codes[i][:, cols].bitcast(FP8X4),
                lhsT_scale=w_bytes[i][:, cols],
                rhs=x_codes[o][:, entries].bitcast(FP8X4),
                rhs_scale=x_bytes[4 * o :, entries],
                start=(o == 0),
                stop=(o == PASSES - 1),
            )

        def product(i):
            acc = sums.tile([P, S], F32, name=f"acc{i}", tag=f"bank{(i + 1) % 3}")
            for o in range(PASSES):
                mx_pass(acc[:], i, o, slice(0, S))
            return acc

        def silu(i, acc, home=None):
            y = sbuf([P, S], F32, f"y{i}", home)
            nc.scalar.activation(y[:], acc[:], ACT.Silu, bias=bias[:, i : i + 1])
            return y

        def fetch(i, y, home):
            terms = []
            for d in range(D):
                term = sbuf([P, V], F32, f"term{i}_{d}", home.get(d))
                nc.vector.tensor_tensor(term[:], y[:].indirect(nbr_lists[d][:]), gates[:, d, :], ALU.mult)
                terms.append(term)
            return terms

        def add_on_vector(i, terms):
            cols = [slice(h * P, (h + 1) * P) for h in range(HALVES)]
            part = sbuf([P, V], F32, f"part{i}")
            for c in cols:
                nc.vector.tensor_tensor(part[:, c], terms[0][:, c], terms[1][:, c], ALU.add)
            res = sbuf([P, V], F32, f"res{i}")
            for c in cols:
                nc.vector.tensor_tensor(res[:, c], part[:, c], terms[2][:, c], ALU.add)
                nc.sync.dma_start(out[i * P : (i + 1) * P, c], res[:, c])

        def add_on_tensor(i, terms):
            turned = (sums.tile([P, HALVES, P], F32, name=f"turned{i}", tag="bank2") if i == 0 else turns.tile([P, HALVES, P], F32, name=f"turned{i}", tag="turns"))
            for h in range(HALVES):
                for d in range(D):
                    nc.tensor.matmul(
                        turned[:, h, :],
                        terms[d][:, h * P : (h + 1) * P],
                        ident[:],
                        is_transpose=True,
                        start=(d == 0),
                        stop=(d == D - 1),
                    )
            staged = sbuf([P, HALVES, P], F32, f"staged{i}")
            nc.scalar.copy(staged[:], turned[:])
            back = turns.tile([P, V], F32, name=f"back{i}", tag="turns")
            for h in range(HALVES):
                nc.tensor.transpose(back[:, h * P : (h + 1) * P], staged[:, h, :], ident[:])
            res = sbuf([P, V], F32, f"res{i}")
            nc.scalar.copy(res[:], back[:])
            nc.sync.dma_start(out[i * P : (i + 1) * P, :], res[:])

        for o in range(PASSES):
            cast_w(0, o, nc.scalar.copy)
        quantize_w(0)
        nc.vector.tensor_copy(x_codes[0][:], x_tab[0][:].bitcast(U32).indirect(node_list[:]))
        nc.vector.tensor_copy(x_bytes[:], s_tab[:].indirect(node_list[:]))

        bias_t = turns.tile([P, P], F32, name="bias_t", tag="turns")
        nc.tensor.transpose(bias_t[:], bias_rows[:], ident[:])
        bias = sbuf([P, BLOCKS], F32, "bias")
        nc.scalar.copy(bias[:], bias_t[:, 0:BLOCKS])

        half = S // 2
        first = [sums.tile([P, half], F32, name=f"first{u}", tag=f"bank{u}") for u in range(2)]
        for u in range(2):
            mx_pass(first[u][:], 0, 0, slice(u * half, (u + 1) * half))
        y0 = sbuf([P, S], F32, "y0")
        for u in range(2):
            entries = slice(u * half, (u + 1) * half)
            nc.vector.tensor_copy(
                x_codes[1][:, entries],
                x_tab[1][:].bitcast(U32).indirect(node_list[:, u * half // 16 : (u + 1) * half // 16]),
            )
            mx_pass(first[u][:], 0, 1, entries)
            nc.scalar.activation(y0[:, entries], first[u][:], ACT.Silu, bias=bias[:, 0:1])
        cast_w(1, 0, nc.scalar.copy)
        cast_w(1, 1, nc.vector.tensor_copy)
        quantize_w(1)
        acc1 = product(1)

        for o in range(PASSES):
            cast_w(2, o, nc.scalar.copy)
        y1 = silu(1, acc1, "w_raw2_1")
        terms0 = fetch(0, y0, {0: homes[1]})
        quantize_w(2)
        acc2 = product(2)
        for o in range(PASSES):
            cast_w(3, o, nc.scalar.copy)
        quantize_w(3)
        y2 = silu(2, acc2)
        acc3 = product(3)
        terms1 = fetch(1, y1, {0: homes[2], 2: homes[3]})
        y3 = silu(3, acc3)
        add_on_tensor(0, terms0)
        terms2 = fetch(2, y2, {})
        add_on_tensor(1, terms1)
        terms3 = fetch(3, y3, {})
        add_on_tensor(2, terms2)
        add_on_vector(3, terms3)
